import numpy as np
import ml_dtypes


def mxq(x, axis, fmt="e4m3"):
    dtype, down = {"e4m3": (ml_dtypes.float8_e4m3fn, 7), "e5m2": (ml_dtypes.float8_e5m2, 14)}[fmt]
    v = np.moveaxis(np.asarray(x, np.float32).astype(ml_dtypes.bfloat16).astype(np.float64), axis, -1)
    blocks = v.reshape(v.shape[:-1] + (-1, 32))
    amax = np.abs(blocks).max(-1, keepdims=True)
    byte = np.maximum(np.where(amax > 0, np.frexp(amax)[1] - 1 + 127, 0) - down, 1)
    scale = np.exp2(byte - 127.0)
    codes = (blocks / scale).astype(np.float32).astype(dtype).astype(np.float64)
    return np.moveaxis((codes * scale).reshape(v.shape), -1, axis)


WIDE = False


def mx_kscale(k):
    if not WIDE:
        return np.ones(k)
    levels = np.array([10, -10, 5, -5, 0])
    if k % 512:
        return np.exp2(np.random.permutation(np.resize(levels, k // 32))).repeat(32)
    a = np.empty((k // 512, 16))
    for p in range(k // 512):
        a[p, :8] = np.random.permutation(np.resize(levels, 8))
        for g in range(8):
            far = levels[np.abs(levels - a[p, g]) >= 10]
            a[p, g + 8] = far[np.random.randint(len(far))]
    return np.exp2(a.ravel()).repeat(32)


def f64(x):
    return np.asarray(x).astype(np.float64)


def striped(idx):
    return np.tile(idx.reshape(-1, 16).T, (8, 1)).astype(np.uint16)


def unstriped(offs):
    return offs[:16].T.reshape(-1).astype(np.int64)


def pack_weight(w):
    k, n = w.shape
    w = f64(np.asarray(w, np.float32).astype(ml_dtypes.bfloat16)).reshape(k // 32, 32, n)
    amax = np.abs(w).max(1)
    byte = np.clip(np.where(amax > 0, np.frexp(amax)[1] - 1 + 127 - 7, 1), 1, 254)
    scaled = (w * np.exp2(127.0 - byte)[:, None, :]).reshape(k, n).astype(np.float32)
    words = np.ascontiguousarray(scaled.reshape(k // 512, 128, 4, n).transpose(0, 1, 3, 2)).astype(ml_dtypes.float8_e4m3fn).view(np.uint8)
    return words, np.ascontiguousarray(byte.astype(np.uint8).reshape(k // 512, 16, n))


def unpack_weight(words, scales):
    g, p, n, _ = words.shape
    vals = np.ascontiguousarray(words).view(ml_dtypes.float8_e4m3fn).astype(np.float64) * np.repeat(np.exp2(scales.astype(np.float64) - 127.0), 8, axis=1)[..., None]
    return vals.transpose(0, 1, 3, 2).reshape(g * 512, n)


def relu(v):
    return np.maximum(v, 0.0)


def sigmoid(v):
    return 1.0 / (1.0 + np.exp(-np.maximum(v, -700.0)))


K, T, S, V, N = 512, 2048, 1024, 512, 256


def setup_inputs():
    n = np.random.standard_normal
    s = mx_kscale(K)[:, None]
    packed_w1 = pack_weight(n((K, N)) / np.sqrt(K) / s)
    packed_w2 = pack_weight(n((K, N)) / np.sqrt(K) / s)
    packed_w3 = pack_weight(n((K, N)) / np.sqrt(K) / s)
    return {
        "xT": (n((K, T)) * s).astype(np.float32),
        "w1_words": packed_w1[0],
        "w1_scales": packed_w1[1],
        "w2_words": packed_w2[0],
        "w2_scales": packed_w2[1],
        "w3_words": packed_w3[0],
        "w3_scales": packed_w3[1],
        "offs": striped(np.random.permutation(T)[:S]),
        "cen": striped(np.random.permutation(S)[:V]),
        "pos1": striped(np.random.permutation(S)[:V]),
        "pos2": striped(np.random.permutation(S)[:V]),
        "pos3": striped(np.random.permutation(S)[:V]),
        "pos4": striped(np.random.permutation(S)[:V]),
    }


def reference(xT, w1_words, w1_scales, w2_words, w2_scales, w3_words, w3_scales, offs, cen, pos1, pos2, pos3, pos4):
    xq = mxq(f64(xT)[:, unstriped(offs)], 0, "e4m3")
    y = unpack_weight(w1_words, w1_scales).T @ xq
    yc = y[:, unstriped(cen)]
    e = unpack_weight(w2_words, w2_scales).T @ xq
    h = unpack_weight(w3_words, w3_scales).T @ xq
    z = (sigmoid(yc + e[:, unstriped(pos1)])) * h[:, unstriped(pos1)] + (sigmoid(yc + e[:, unstriped(pos2)])) * h[:, unstriped(pos2)] + (sigmoid(yc + e[:, unstriped(pos3)])) * h[:, unstriped(pos3)] + (sigmoid(yc + e[:, unstriped(pos4)])) * h[:, unstriped(pos4)]
    return relu(z)

@@ -1,0 +1,223 @@
+from contextlib import ExitStack
+
+import concourse.mybir as mybir
+from concourse.masks import make_identity
+
+K, T, S, V, N = 512, 2048, 1024, 512, 256
+FLOPS = 3 * 2 * K * N * S
+
+F32 = mybir.dt.float32
+BF16 = mybir.dt.bfloat16
+U32 = mybir.dt.uint32
+I32 = mybir.dt.int32
+U16 = mybir.dt.uint16
+U8 = mybir.dt.uint8
+FP8X4 = mybir.dt.float8_e4m3fn_x4
+ADD = mybir.AluOpType.add
+MULT = mybir.AluOpType.mult
+ACT = mybir.ActivationFunctionType
+
+P = 128
+BANK = 512
+PIECE = 256
+PIECES = S // PIECE
+LIST_COLS = 16
+
+
+def tile_picked_gatedg_relu_e_kernel(
+    tc, xT, w1_words, w1_scales, w2_words, w2_scales, w3_words, w3_scales, offs, cen, pos1, pos2, pos3, pos4, out
+):
+    nc = tc.nc
+    with ExitStack() as ctx:
+        keep = ctx.enter_context(tc.tile_pool(name="keep", bufs=1))
+        psum = ctx.enter_context(tc.psum_pool(name="psum", bufs=8))
+
+        def load_list(name, src):
+            t = keep.tile(list(src.shape), U16, name=name)
+            nc.sync.dma_start(t[:], src)
+            return t
+
+        w_scales = keep.tile([P, 3 * N], U8, name="w_scales", align_bytes=64)
+        nc.gpsimd.memset(w_scales[:].bitcast(I32), 0)
+        ident = keep.tile([P, P], F32, name="ident")
+        make_identity(nc, ident[:])
+
+        x_rows = xT.rearrange("(p j) t -> p j t", j=4)
+
+        def load_x(u, t0, t1):
+            raw = keep.tile([P, 2, t1 - t0], F32, name="raw_%d_%d" % (u, t0))
+            nc.sync.dma_start(raw[:], x_rows[:, 2 * u : 2 * u + 2, t0:t1])
+            return raw
+
+        raw_a = [load_x(0, 0, 1024)]
+        offs_t = load_list("offs_t", offs)
+        raw_a.append(load_x(0, 1024, 2048))
+        for j, src in enumerate((w1_scales, w2_scales, w3_scales)):
+            nc.sync.dma_start(w_scales[0:16, j * N : (j + 1) * N].bitcast(I32), src[0].bitcast(I32))
+        raw_b = [load_x(1, 512 * c, 512 * (c + 1)) for c in range(4)]
+        for q in range(1, 4):
+            nc.sync.dma_start(w_scales[32 * q : 32 * q + 4, :].bitcast(I32), w_scales[4 * q : 4 * q + 4, :].bitcast(I32))
+        w_words = []
+        for j, src in enumerate((w1_words, w2_words, w3_words)):
+            t = keep.tile([P, N], U32, name="w_words%d" % j, align_bytes=64)
+            nc.sync.dma_start(t[:].bitcast(I32), src[0].rearrange("p n t -> p (n t)").bitcast(I32))
+            w_words.append(t)
+        cen_t = load_list("cen_t", cen)
+        pos_t = [load_list("pos%d_t" % d, src) for d, src in enumerate((pos1, pos2, pos3, pos4))]
+
+        pairs = [keep.tile([P, T], U32, name="pairs%d" % u) for u in range(2)]
+
+        def cast(copy, u, raw, t0, c0, c1):
+            dst = pairs[u][:, t0 + c0 : t0 + c1].bitcast(BF16).rearrange("p (t j) -> p t j", j=2)
+            copy(dst, raw[:, :, c0:c1].rearrange("p j t -> p t j"))
+
+        picked = [keep.tile([P, 2, PIECE], U32, name="picked%d" % i) for i in range(PIECES)]
+
+        def pick(u, i):
+            cols = PIECE // LIST_COLS
+            nc.vector.tensor_copy(picked[i][:, u, :], pairs[u][:].indirect(offs_t[:, i * cols : (i + 1) * cols]))
+
+        cast(nc.vector.tensor_copy, 0, raw_a[0], 0, 0, 1024)
+        cast(nc.vector.tensor_copy, 0, raw_a[1], 1024, 0, 1024)
+        cast(nc.scalar.copy, 1, raw_b[0], 0, 0, 512)
+        cast(nc.scalar.copy, 1, raw_b[1], 512, 0, 512)
+        for i in range(PIECES):
+            pick(0, i)
+        cast(nc.vector.tensor_copy, 1, raw_b[2], 1024, 0, 512)
+        cast(nc.vector.tensor_copy, 1, raw_b[3], 1536, 0, 320)
+        cast(nc.scalar.copy, 1, raw_b[3], 1536, 320, 512)
+
+        x_words = keep.tile([P, S], U32, name="x_words", align_bytes=64)
+        x_scales = keep.tile([P, S], U8, name="x_scales", align_bytes=64)
+        woven = [keep.tile([P, PIECE, 2], U32, name="woven%d" % i, align_bytes=64) for i in range(PIECES)]
+
+        def product(bank, j, b, c0, c1):
+            m0 = b * P
+            nc.tensor.matmul_mx(
+                out=bank[:, c0 % BANK : c0 % BANK + c1 - c0],
+                lhsT=w_words[j][:, m0 : m0 + P].bitcast(FP8X4),
+                lhsT_scale=w_scales[:, j * N + m0 : j * N + m0 + P],
+                rhs=x_words[:, c0:c1].bitcast(FP8X4),
+                rhs_scale=x_scales[:, c0:c1],
+                start=True,
+                stop=True,
+            )
+
+        def new_bank(name):
+            return psum.tile([P, BANK], F32, name=name, tag="bank")
+
+        banks0 = [[new_bank("acc0_%d_%d" % (j, hf)) for hf in range(2)] for j in range(3)]
+
+        def quantise(i):
+            cols = slice(i * PIECE, (i + 1) * PIECE)
+            nc.vector.quantize_mx(
+                out=x_words[:, cols].bitcast(FP8X4),
+                scales=x_scales[:, cols],
+                in_=woven[i][:].rearrange("p n u -> p (n u)").bitcast(BF16),
+            )
+            for j in range(3):
+                product(banks0[j][i * PIECE // BANK], j, 0, i * PIECE, (i + 1) * PIECE)
+
+        for i in range(PIECES):
+            pick(1, i)
+            nc.scalar.copy(woven[i][:], picked[i][:].rearrange("p u n -> p n u"))
+            if i >= 1:
+                quantise(i - 1)
+        quantise(PIECES - 1)
+
+        rows = [[keep.tile([P, S], F32, name="rows%d_%d" % (b, j)) for j in range(3)] for b in range(2)]
+
+        def empty(copy, b, j, hf, bank):
+            copy(rows[b][j][:, hf * BANK : (hf + 1) * BANK], bank[:])
+
+        empty(nc.scalar.copy, 0, 1, 0, banks0[1][0])
+        empty(nc.vector.tensor_copy, 0, 0, 0, banks0[0][0])
+        empty(nc.scalar.copy, 0, 0, 1, banks0[0][1])
+        empty(nc.scalar.copy, 0, 1, 1, banks0[1][1])
+        empty(nc.scalar.copy, 0, 2, 0, banks0[2][0])
+        empty(nc.scalar.copy, 0, 2, 1, banks0[2][1])
+
+        def products1(j):
+            for hf in range(2):
+                bank = new_bank("acc1_%d_%d" % (j, hf))
+                product(bank, j, 1, hf * BANK, (hf + 1) * BANK)
+                empty(nc.scalar.copy, 1, j, hf, bank)
+
+        def gates(b):
+            yc = keep.tile([P, V], F32, name="yc%d" % b)
+            nc.vector.tensor_copy(yc[:], rows[b][0][:].indirect(cen_t[:]))
+            res = []
+            for d in range(4):
+                pre = keep.tile([P, V], F32, name="pre%d_%d" % (b, d))
+                nc.vector.tensor_tensor(pre[:], rows[b][1][:].indirect(pos_t[d][:]), yc[:], ADD)
+                if b == 1 and d == 2:
+                    gate = keep.tile([P, V], F32, name="gate%d_%d" % (b, d), tag="late")
+                else:
+                    gate = keep.tile([P, V], F32, name="gate%d_%d" % (b, d))
+                nc.scalar.activation(gate[:], pre[:], ACT.Sigmoid)
+                res.append(gate)
+            return res
+
+        def message(b, d, gate, msg, v0, v1):
+            lst = pos_t[d][:, v0 // LIST_COLS : v1 // LIST_COLS]
+            nc.vector.tensor_tensor(msg[:, v0:v1], rows[b][2][:].indirect(lst), gate[:, v0:v1], MULT)
+
+        def add_turned(bank, src, first, last):
+            for c in range(V // P):
+                nc.tensor.matmul(
+                    bank[:, c * P : (c + 1) * P],
+                    src[:, c * P : (c + 1) * P],
+                    ident[:],
+                    start=(first and c == 0),
+                    stop=(last and c == V // P - 1),
+                    is_transpose=True,
+                )
+
+        def turn_back(name, src):
+            bank = new_bank(name)
+            for c in range(V // P):
+                nc.tensor.transpose(bank[:, c * P : (c + 1) * P], src[:, c * P : (c + 1) * P], ident[:])
+            return bank
+
+        gates0 = gates(0)
+        products1(0)
+        products1(1)
+        sum0 = new_bank("sum0")
+        for d in range(3):
+            msg = keep.tile([P, V], F32, name="msg0_%d" % d)
+            message(0, d, gates0[d], msg, 0, V)
+            add_turned(sum0, msg, d == 0, False)
+        products1(2)
+        gates1 = gates(1)
+        sum1 = new_bank("sum1")
+        for d in range(3):
+            msg = keep.tile([P, V], F32, name="msg1_%d" % d)
+            message(1, d, gates1[d], msg, 0, V)
+            add_turned(sum1, msg, d == 0, d == 2)
+        part_t = keep.tile([P, V], F32, name="part_t")
+        nc.scalar.copy(part_t[:], sum1[:])
+        part = turn_back("part", part_t)
+
+        msg = keep.tile([P, V], F32, name="msg0_3", tag="late")
+        message(0, 3, gates0[3], msg, 0, V)
+        add_turned(sum0, msg, False, True)
+        out0_t = keep.tile([P, V], F32, name="out0_t")
+        nc.scalar.activation(out0_t[:], sum0[:], ACT.Relu)
+        back0 = turn_back("back0", out0_t)
+
+        half = V // 2
+        last = keep.tile([P, V], F32, name="last")
+        z = keep.tile([P, V], F32, name="z")
+        res1 = keep.tile([P, V], F32, name="res1")
+        for hf in range(2):
+            message(1, 3, gates1[3], last, hf * half, (hf + 1) * half)
+        for hf in range(2):
+            cols = slice(hf * half, (hf + 1) * half)
+            nc.vector.tensor_tensor(z[:, cols], last[:, cols], part[:, cols], ADD)
+        nc.scalar.activation(res1[:, 0:half], z[:, 0:half], ACT.Relu)
+        nc.sync.dma_start(out[P : 2 * P, 0:half], res1[:, 0:half])
+        res0 = keep.tile([P, V], F32, name="res0")
+        nc.scalar.copy(res0[:], back0[:])
+        nc.vector.tensor_scalar_max(res1[:, half:V], z[:, half:V], 0.0)
+        nc.sync.dma_start(out[P : 2 * P, half:V], res1[:, half:V])
+        nc.sync.dma_start(out[0:P, :], res0[:])

@@ -30,7 +30,7 @@ def tile_picked_gatedg_relu_e_kernel(
     nc = tc.nc
     with ExitStack() as ctx:
         keep = ctx.enter_context(tc.tile_pool(name="keep", bufs=1))
-        psum = ctx.enter_context(tc.psum_pool(name="psum", bufs=8))
+        psum = ctx.enter_context(tc.psum_pool(name="psum", bufs=1))
 
         def load_list(name, src):
             t = keep.tile(list(src.shape), U16, name=name)
@@ -38,7 +38,12 @@ def tile_picked_gatedg_relu_e_kernel(
             return t
 
         w_scales = keep.tile([P, 3 * N], U8, name="w_scales", align_bytes=64)
-        nc.gpsimd.memset(w_scales[:].bitcast(I32), 0)
+        staged = keep.tile([16, 3 * N // 4], I32, name="staged")
+        for j, src in enumerate((w1_scales, w2_scales, w3_scales)):
+            nc.scalar.dma_start(staged[:, j * N // 4 : (j + 1) * N // 4], src[0].bitcast(I32))
+        nc.vector.memset(w_scales[:].bitcast(I32), 0)
+        for q in range(4):
+            nc.gpsimd.dma_start(w_scales[32 * q : 32 * q + 4, :].bitcast(I32), staged[4 * q : 4 * q + 4, :])
         ident = keep.tile([P, P], F32, name="ident")
         make_identity(nc, ident[:])
 
@@ -52,11 +57,8 @@ def tile_picked_gatedg_relu_e_kernel(
         raw_a = [load_x(0, 0, 1024)]
         offs_t = load_list("offs_t", offs)
         raw_a.append(load_x(0, 1024, 2048))
-        for j, src in enumerate((w1_scales, w2_scales, w3_scales)):
-            nc.sync.dma_start(w_scales[0:16, j * N : (j + 1) * N].bitcast(I32), src[0].bitcast(I32))
-        raw_b = [load_x(1, 512 * c, 512 * (c + 1)) for c in range(4)]
-        for q in range(1, 4):
-            nc.sync.dma_start(w_scales[32 * q : 32 * q + 4, :].bitcast(I32), w_scales[4 * q : 4 * q + 4, :].bitcast(I32))
+        b_cuts = (0, 512, 1024, 1536, 1792, 2048)
+        raw_b = [load_x(1, b_cuts[c], b_cuts[c + 1]) for c in range(5)]
         w_words = []
         for j, src in enumerate((w1_words, w2_words, w3_words)):
             t = keep.tile([P, N], U32, name="w_words%d" % j, align_bytes=64)
@@ -71,30 +73,33 @@ def tile_picked_gatedg_relu_e_kernel(
             dst = pairs[u][:, t0 + c0 : t0 + c1].bitcast(BF16).rearrange("p (t j) -> p t j", j=2)
             copy(dst, raw[:, :, c0:c1].rearrange("p j t -> p t j"))
 
-        picked = [keep.tile([P, 2, PIECE], U32, name="picked%d" % i) for i in range(PIECES)]
+        picked = [keep.tile([P, 2 * PIECE], U32, name="picked%d" % i) for i in range(PIECES)]
 
         def pick(u, i):
             cols = PIECE // LIST_COLS
-            nc.vector.tensor_copy(picked[i][:, u, :], pairs[u][:].indirect(offs_t[:, i * cols : (i + 1) * cols]))
+            nc.vector.tensor_copy(picked[i][:, u * PIECE : (u + 1) * PIECE], pairs[u][:].indirect(offs_t[:, i * cols : (i + 1) * cols]))
 
         cast(nc.vector.tensor_copy, 0, raw_a[0], 0, 0, 1024)
-        cast(nc.vector.tensor_copy, 0, raw_a[1], 1024, 0, 1024)
+        cast(nc.vector.tensor_copy, 0, raw_a[1], 1024, 0, 704)
+        cast(nc.scalar.copy, 0, raw_a[1], 1024, 704, 1024)
         cast(nc.scalar.copy, 1, raw_b[0], 0, 0, 512)
         cast(nc.scalar.copy, 1, raw_b[1], 512, 0, 512)
         for i in range(PIECES):
             pick(0, i)
-        cast(nc.vector.tensor_copy, 1, raw_b[2], 1024, 0, 512)
-        cast(nc.vector.tensor_copy, 1, raw_b[3], 1536, 0, 320)
-        cast(nc.scalar.copy, 1, raw_b[3], 1536, 320, 512)
+        cast(nc.vector.tensor_copy, 1, raw_b[2], 1024, 0, 256)
+        cast(nc.scalar.copy, 1, raw_b[2], 1024, 256, 512)
+        cast(nc.vector.tensor_copy, 1, raw_b[3], 1536, 0, 256)
+        cast(nc.vector.tensor_copy, 1, raw_b[4], 1792, 0, 160)
+        cast(nc.scalar.copy, 1, raw_b[4], 1792, 160, 256)
 
         x_words = keep.tile([P, S], U32, name="x_words", align_bytes=64)
         x_scales = keep.tile([P, S], U8, name="x_scales", align_bytes=64)
-        woven = [keep.tile([P, PIECE, 2], U32, name="woven%d" % i, align_bytes=64) for i in range(PIECES)]
+        woven = [keep.tile([P, 2 * PIECE], U32, name="woven%d" % i, align_bytes=64) for i in range(PIECES)]
 
         def product(bank, j, b, c0, c1):
             m0 = b * P
             nc.tensor.matmul_mx(
-                out=bank[:, c0 % BANK : c0 % BANK + c1 - c0],
+                out=bank,
                 lhsT=w_words[j][:, m0 : m0 + P].bitcast(FP8X4),
                 lhsT_scale=w_scales[:, j * N + m0 : j * N + m0 + P],
                 rhs=x_words[:, c0:c1].bitcast(FP8X4),
@@ -103,57 +108,58 @@ def tile_picked_gatedg_relu_e_kernel(
                 stop=True,
             )
 
-        def new_bank(name):
-            return psum.tile([P, BANK], F32, name=name, tag="bank")
+        def new_bank(name, tag):
+            return psum.tile([P, BANK], F32, name=name, tag="bank%d" % tag)
 
-        banks0 = [[new_bank("acc0_%d_%d" % (j, hf)) for hf in range(2)] for j in range(3)]
-
-        def quantise(i):
-            cols = slice(i * PIECE, (i + 1) * PIECE)
+        def quantise(c0, c1):
+            i = c0 // PIECE
             nc.vector.quantize_mx(
-                out=x_words[:, cols].bitcast(FP8X4),
-                scales=x_scales[:, cols],
-                in_=woven[i][:].rearrange("p n u -> p (n u)").bitcast(BF16),
+                out=x_words[:, c0:c1].bitcast(FP8X4),
+                scales=x_scales[:, c0:c1],
+                in_=woven[i][:, 2 * (c0 - i * PIECE) : 2 * (c1 - i * PIECE)].bitcast(BF16),
             )
-            for j in range(3):
-                product(banks0[j][i * PIECE // BANK], j, 0, i * PIECE, (i + 1) * PIECE)
 
-        for i in range(PIECES):
+        def pick_and_weave(i):
             pick(1, i)
-            nc.scalar.copy(woven[i][:], picked[i][:].rearrange("p u n -> p n u"))
-            if i >= 1:
-                quantise(i - 1)
-        quantise(PIECES - 1)
+            nc.scalar.copy(woven[i][:].rearrange("p (n u) -> p n u", u=2), picked[i][:].rearrange("p (u n) -> p n u", u=2))
 
         rows = [[keep.tile([P, S], F32, name="rows%d_%d" % (b, j)) for j in range(3)] for b in range(2)]
 
-        def empty(copy, b, j, hf, bank):
-            copy(rows[b][j][:, hf * BANK : (hf + 1) * BANK], bank[:])
+        def product_rows(b, j, c0, c1, tag, copy=nc.scalar.copy):
+            bank = new_bank("acc%d_%d_%d" % (b, j, c0), tag)
+            product(bank[:, 0 : c1 - c0], j, b, c0, c1)
+            copy(rows[b][j][:, c0:c1], bank[:, 0 : c1 - c0])
 
-        empty(nc.scalar.copy, 0, 1, 0, banks0[1][0])
-        empty(nc.vector.tensor_copy, 0, 0, 0, banks0[0][0])
-        empty(nc.scalar.copy, 0, 0, 1, banks0[0][1])
-        empty(nc.scalar.copy, 0, 1, 1, banks0[1][1])
-        empty(nc.scalar.copy, 0, 2, 0, banks0[2][0])
-        empty(nc.scalar.copy, 0, 2, 1, banks0[2][1])
+        for i in range(PIECES):
+            pick_and_weave(i)
+        cuts = (0, PIECE, 2 * PIECE, 3 * PIECE, S - P, S)
+        for c0, c1 in zip(cuts, cuts[1:]):
+            quantise(c0, c1)
+        product_rows(0, 0, 0, PIECE, 0)
+        product_rows(0, 0, PIECE, 2 * PIECE, 7)
+        product_rows(0, 0, 2 * PIECE, 3 * PIECE, 1, nc.vector.tensor_copy)
+        product_rows(0, 0, 3 * PIECE, S - P, 4)
+        product_rows(0, 0, S - P, S, 2)
+        product_rows(0, 1, BANK, S, 3)
+        product_rows(0, 1, 0, BANK, 1)
+        product_rows(0, 2, 0, BANK, 2)
+        product_rows(0, 2, BANK, S, 3)
 
         def products1(j):
             for hf in range(2):
-                bank = new_bank("acc1_%d_%d" % (j, hf))
-                product(bank, j, 1, hf * BANK, (hf + 1) * BANK)
-                empty(nc.scalar.copy, 1, j, hf, bank)
+                product_rows(1, j, hf * BANK, (hf + 1) * BANK, 1 + (2 * j + hf) % 3)
 
-        def gates(b):
+        def centre(b):
             yc = keep.tile([P, V], F32, name="yc%d" % b)
             nc.vector.tensor_copy(yc[:], rows[b][0][:].indirect(cen_t[:]))
+            return yc
+
+        def gates(b, yc):
             res = []
             for d in range(4):
                 pre = keep.tile([P, V], F32, name="pre%d_%d" % (b, d))
                 nc.vector.tensor_tensor(pre[:], rows[b][1][:].indirect(pos_t[d][:]), yc[:], ADD)
-                if b == 1 and d == 2:
-                    gate = keep.tile([P, V], F32, name="gate%d_%d" % (b, d), tag="late")
-                else:
-                    gate = keep.tile([P, V], F32, name="gate%d_%d" % (b, d))
+                gate = keep.tile([P, V], F32, name="gate%d_%d" % (b, d))
                 nc.scalar.activation(gate[:], pre[:], ACT.Sigmoid)
                 res.append(gate)
             return res
@@ -162,62 +168,79 @@ def tile_picked_gatedg_relu_e_kernel(
             lst = pos_t[d][:, v0 // LIST_COLS : v1 // LIST_COLS]
             nc.vector.tensor_tensor(msg[:, v0:v1], rows[b][2][:].indirect(lst), gate[:, v0:v1], MULT)
 
-        def add_turned(bank, src, first, last):
-            for c in range(V // P):
+        def add_turned(bank, src, v0, v1, first, last):
+            for c in range(v0, v1, P):
                 nc.tensor.matmul(
-                    bank[:, c * P : (c + 1) * P],
-                    src[:, c * P : (c + 1) * P],
+                    bank[:, c - v0 : c - v0 + P],
+                    src[:, c : c + P],
                     ident[:],
-                    start=(first and c == 0),
-                    stop=(last and c == V // P - 1),
+                    start=(first and c == v0),
+                    stop=(last and c + P == v1),
                     is_transpose=True,
                 )
 
-        def turn_back(name, src):
-            bank = new_bank(name)
-            for c in range(V // P):
-                nc.tensor.transpose(bank[:, c * P : (c + 1) * P], src[:, c * P : (c + 1) * P], ident[:])
+        def turn_back(name, src, width, tag):
+            bank = new_bank(name, tag)
+            for c in range(0, width, P):
+                nc.tensor.transpose(bank[:, c : c + P], src[:, c : c + P], ident[:])
             return bank
 
-        gates0 = gates(0)
+        gates0 = gates(0, centre(0))
         products1(0)
         products1(1)
-        sum0 = new_bank("sum0")
-        for d in range(3):
+        sum0 = new_bank("sum0", 0)
+        for d in range(4):
             msg = keep.tile([P, V], F32, name="msg0_%d" % d)
             message(0, d, gates0[d], msg, 0, V)
-            add_turned(sum0, msg, d == 0, False)
-        products1(2)
-        gates1 = gates(1)
-        sum1 = new_bank("sum1")
-        for d in range(3):
-            msg = keep.tile([P, V], F32, name="msg1_%d" % d)
-            message(1, d, gates1[d], msg, 0, V)
-            add_turned(sum1, msg, d == 0, d == 2)
-        part_t = keep.tile([P, V], F32, name="part_t")
-        nc.scalar.copy(part_t[:], sum1[:])
-        part = turn_back("part", part_t)
-
-        msg = keep.tile([P, V], F32, name="msg0_3", tag="late")
-        message(0, 3, gates0[3], msg, 0, V)
-        add_turned(sum0, msg, False, True)
+            add_turned(sum0, msg, 0, V, d == 0, d == 3)
+            if d == 0:
+                products1(2)
+            if d == 2:
+                yc1 = centre(1)
+        gates1 = gates(1, yc1)
         out0_t = keep.tile([P, V], F32, name="out0_t")
         nc.scalar.activation(out0_t[:], sum0[:], ACT.Relu)
-        back0 = turn_back("back0", out0_t)
-
-        half = V // 2
-        last = keep.tile([P, V], F32, name="last")
-        z = keep.tile([P, V], F32, name="z")
-        res1 = keep.tile([P, V], F32, name="res1")
-        for hf in range(2):
-            message(1, 3, gates1[3], last, hf * half, (hf + 1) * half)
-        for hf in range(2):
-            cols = slice(hf * half, (hf + 1) * half)
-            nc.vector.tensor_tensor(z[:, cols], last[:, cols], part[:, cols], ADD)
-        nc.scalar.activation(res1[:, 0:half], z[:, 0:half], ACT.Relu)
-        nc.sync.dma_start(out[P : 2 * P, 0:half], res1[:, 0:half])
+        back0 = turn_back("back0", out0_t, V, 6)
         res0 = keep.tile([P, V], F32, name="res0")
         nc.scalar.copy(res0[:], back0[:])
-        nc.vector.tensor_scalar_max(res1[:, half:V], z[:, half:V], 0.0)
-        nc.sync.dma_start(out[P : 2 * P, half:V], res1[:, half:V])
         nc.sync.dma_start(out[0:P, :], res0[:])
+
+        half = V // 2
+        sum_l = [new_bank("sum_l%d" % c, 4 + c) for c in range(2)]
+        sum_r = new_bank("sum_r", 7)
+        msgs = [keep.tile([P, V], F32, name="msg1_%d" % d) for d in range(4)]
+
+        def add_left(d):
+            for c in range(2):
+                add_turned(sum_l[c], msgs[d], c * P, (c + 1) * P, d == 0, d == 3)
+
+        for d in range(2):
+            message(1, d, gates1[d], msgs[d], 0, V)
+            add_turned(sum_r, msgs[d], half, V, d == 0, False)
+            add_left(d)
+        message(1, 2, gates1[2], msgs[2], half, V)
+        add_turned(sum_r, msgs[2], half, V, False, True)
+        part_t = keep.tile([P, half], F32, name="part_t")
+        nc.scalar.copy(part_t[:], sum_r[:, 0:half])
+        part = turn_back("part", part_t, half, 1)
+        for d in range(2, 4):
+            message(1, d, gates1[d], msgs[d], 0, half)
+            add_left(d)
+        res_l = keep.tile([P, half], F32, name="res_l")
+        left = []
+        for c in range(2):
+            left_t = keep.tile([P, P], F32, name="left_t%d" % c)
+            nc.scalar.activation(left_t[:], sum_l[c][:, 0:P], ACT.Relu)
+            left.append(turn_back("left%d" % c, left_t, P, 2 + c))
+        for c in range(2):
+            nc.scalar.copy(res_l[:, c * P : (c + 1) * P], left[c][:, 0:P])
+        nc.scalar.dma_start(out[P : 2 * P, 0:half], res_l[:])
+        for c in range(2):
+            message(1, 3, gates1[3], msgs[3], half + c * P, half + (c + 1) * P)
+        z = keep.tile([P, half], F32, name="z")
+        res_r = keep.tile([P, half], F32, name="res_r")
+        for c in range(2):
+            cols = slice(c * P, (c + 1) * P)
+            nc.vector.tensor_tensor(z[:, cols], msgs[3][:, half + c * P : half + (c + 1) * P], part[:, cols], ADD)
+        nc.vector.tensor_scalar_max(res_r[:], z[:], 0.0)
+        nc.sync.dma_start(out[P : 2 * P, half:V], res_r[:])

@@ -54,9 +54,9 @@ def tile_picked_gatedg_relu_e_kernel(
             nc.sync.dma_start(raw[:], x_rows[:, 2 * u : 2 * u + 2, t0:t1])
             return raw
 
-        raw_a = [load_x(0, 0, 1024)]
+        raw_a = [load_x(0, 0, 1408)]
         offs_t = load_list("offs_t", offs)
-        raw_a.append(load_x(0, 1024, 2048))
+        raw_a.append(load_x(0, 1408, 2048))
         b_cuts = (0, 512, 1024, 1536, 1792, 2048)
         raw_b = [load_x(1, b_cuts[c], b_cuts[c + 1]) for c in range(5)]
         w_words = []
@@ -79,9 +79,10 @@ def tile_picked_gatedg_relu_e_kernel(
             cols = PIECE // LIST_COLS
             nc.vector.tensor_copy(picked[i][:, u * PIECE : (u + 1) * PIECE], pairs[u][:].indirect(offs_t[:, i * cols : (i + 1) * cols]))
 
-        cast(nc.vector.tensor_copy, 0, raw_a[0], 0, 0, 1024)
-        cast(nc.vector.tensor_copy, 0, raw_a[1], 1024, 0, 704)
-        cast(nc.scalar.copy, 0, raw_a[1], 1024, 704, 1024)
+        cast(nc.vector.tensor_copy, 0, raw_a[0], 0, 0, 880)
+        cast(nc.scalar.copy, 0, raw_a[0], 0, 880, 1408)
+        cast(nc.vector.tensor_copy, 0, raw_a[1], 1408, 0, 400)
+        cast(nc.scalar.copy, 0, raw_a[1], 1408, 400, 640)
         cast(nc.scalar.copy, 1, raw_b[0], 0, 0, 512)
         cast(nc.scalar.copy, 1, raw_b[1], 512, 0, 512)
         for i in range(PIECES):
@@ -149,16 +150,22 @@ def tile_picked_gatedg_relu_e_kernel(
             for hf in range(2):
                 product_rows(1, j, hf * BANK, (hf + 1) * BANK, 1 + (2 * j + hf) % 3)
 
-        def centre(b):
+        def centre(b, parts):
             yc = keep.tile([P, V], F32, name="yc%d" % b)
-            nc.vector.tensor_copy(yc[:], rows[b][0][:].indirect(cen_t[:]))
+            for v0 in range(0, V, V // parts):
+                v1 = v0 + V // parts
+                nc.vector.tensor_copy(yc[:, v0:v1], rows[b][0][:].indirect(cen_t[:, v0 // LIST_COLS : v1 // LIST_COLS]))
             return yc
 
         def gates(b, yc):
             res = []
             for d in range(4):
                 pre = keep.tile([P, V], F32, name="pre%d_%d" % (b, d))
-                nc.vector.tensor_tensor(pre[:], rows[b][1][:].indirect(pos_t[d][:]), yc[:], ADD)
+                parts = 2 if (b, d) == (0, 0) else 1
+                for v0 in range(0, V, V // parts):
+                    v1 = v0 + V // parts
+                    lst = pos_t[d][:, v0 // LIST_COLS : v1 // LIST_COLS]
+                    nc.vector.tensor_tensor(pre[:, v0:v1], rows[b][1][:].indirect(lst), yc[:, v0:v1], ADD)
                 gate = keep.tile([P, V], F32, name="gate%d_%d" % (b, d))
                 nc.scalar.activation(gate[:], pre[:], ACT.Sigmoid)
                 res.append(gate)
@@ -185,18 +192,18 @@ def tile_picked_gatedg_relu_e_kernel(
                 nc.tensor.transpose(bank[:, c : c + P], src[:, c : c + P], ident[:])
             return bank
 
-        gates0 = gates(0, centre(0))
+        gates0 = gates(0, centre(0, 2))
         products1(0)
         products1(1)
         sum0 = new_bank("sum0", 0)
         for d in range(4):
-            msg = keep.tile([P, V], F32, name="msg0_%d" % d)
+            msg = keep.tile([P, V], F32, name="msg0_%d" % d, tag="rows1_0" if d == 3 else "msg0_%d" % d)
             message(0, d, gates0[d], msg, 0, V)
             add_turned(sum0, msg, 0, V, d == 0, d == 3)
             if d == 0:
                 products1(2)
             if d == 2:
-                yc1 = centre(1)
+                yc1 = centre(1, 1)
         gates1 = gates(1, yc1)
         out0_t = keep.tile([P, V], F32, name="out0_t")
         nc.scalar.activation(out0_t[:], sum0[:], ACT.Relu)
@@ -242,5 +249,7 @@ def tile_picked_gatedg_relu_e_kernel(
         for c in range(2):
             cols = slice(c * P, (c + 1) * P)
             nc.vector.tensor_tensor(z[:, cols], msgs[3][:, half + c * P : half + (c + 1) * P], part[:, cols], ADD)
-        nc.vector.tensor_scalar_max(res_r[:], z[:], 0.0)
+        for c in range(2):
+            cols = slice(c * P, (c + 1) * P)
+            nc.vector.tensor_scalar_max(res_r[:, cols], z[:, cols], 0.0)
         nc.sync.dma_start(out[P : 2 * P, half:V], res_r[:])

from contextlib import ExitStack

import concourse.mybir as mybir
from concourse.masks import make_identity

K, T, S, V, N = 512, 2048, 1024, 512, 256
FLOPS = 3 * 2 * K * N * S

F32 = mybir.dt.float32
BF16 = mybir.dt.bfloat16
U32 = mybir.dt.uint32
I32 = mybir.dt.int32
U16 = mybir.dt.uint16
U8 = mybir.dt.uint8
FP8X4 = mybir.dt.float8_e4m3fn_x4
ADD = mybir.AluOpType.add
MULT = mybir.AluOpType.mult
ACT = mybir.ActivationFunctionType

P = 128
BANK = 512
PIECE = 256
PIECES = S // PIECE
LIST_COLS = 16


def tile_picked_gatedg_relu_e_kernel(
    tc, xT, w1_words, w1_scales, w2_words, w2_scales, w3_words, w3_scales, offs, cen, pos1, pos2, pos3, pos4, out
):
    nc = tc.nc
    with ExitStack() as ctx:
        keep = ctx.enter_context(tc.tile_pool(name="keep", bufs=1))
        psum = ctx.enter_context(tc.psum_pool(name="psum", bufs=1))

        def load_list(name, src):
            t = keep.tile(list(src.shape), U16, name=name)
            nc.sync.dma_start(t[:], src)
            return t

        w_scales = keep.tile([P, 3 * N], U8, name="w_scales", align_bytes=64)
        staged = keep.tile([16, 3 * N // 4], I32, name="staged")
        for j, src in enumerate((w1_scales, w2_scales, w3_scales)):
            nc.scalar.dma_start(staged[:, j * N // 4 : (j + 1) * N // 4], src[0].bitcast(I32))
        nc.vector.memset(w_scales[:].bitcast(I32), 0)
        for q in range(4):
            nc.gpsimd.dma_start(w_scales[32 * q : 32 * q + 4, :].bitcast(I32), staged[4 * q : 4 * q + 4, :])
        ident = keep.tile([P, P], F32, name="ident")
        make_identity(nc, ident[:])

        x_rows = xT.rearrange("(p j) t -> p j t", j=4)

        def load_x(u, t0, t1):
            raw = keep.tile([P, 2, t1 - t0], F32, name="raw_%d_%d" % (u, t0))
            nc.sync.dma_start(raw[:], x_rows[:, 2 * u : 2 * u + 2, t0:t1])
            return raw

        raw_a = [load_x(0, 0, 1408)]
        offs_t = load_list("offs_t", offs)
        raw_a.append(load_x(0, 1408, 2048))
        b_cuts = (0, 512, 1024, 1536, 1792, 2048)
        raw_b = [load_x(1, b_cuts[c], b_cuts[c + 1]) for c in range(5)]
        w_words = []
        for j, src in enumerate((w1_words, w2_words, w3_words)):
            t = keep.tile([P, N], U32, name="w_words%d" % j, align_bytes=64)
            nc.sync.dma_start(t[:].bitcast(I32), src[0].rearrange("p n t -> p (n t)").bitcast(I32))
            w_words.append(t)
        cen_t = load_list("cen_t", cen)
        pos_t = [load_list("pos%d_t" % d, src) for d, src in enumerate((pos1, pos2, pos3, pos4))]

        pairs = [keep.tile([P, T], U32, name="pairs%d" % u) for u in range(2)]

        def cast(copy, u, raw, t0, c0, c1):
            dst = pairs[u][:, t0 + c0 : t0 + c1].bitcast(BF16).rearrange("p (t j) -> p t j", j=2)
            copy(dst, raw[:, :, c0:c1].rearrange("p j t -> p t j"))

        picked = [keep.tile([P, 2 * PIECE], U32, name="picked%d" % i) for i in range(PIECES)]

        def pick(u, i):
            cols = PIECE // LIST_COLS
            nc.vector.tensor_copy(picked[i][:, u * PIECE : (u + 1) * PIECE], pairs[u][:].indirect(offs_t[:, i * cols : (i + 1) * cols]))

        cast(nc.vector.tensor_copy, 0, raw_a[0], 0, 0, 880)
        cast(nc.scalar.copy, 0, raw_a[0], 0, 880, 1408)
        cast(nc.vector.tensor_copy, 0, raw_a[1], 1408, 0, 400)
        cast(nc.scalar.copy, 0, raw_a[1], 1408, 400, 640)
        cast(nc.scalar.copy, 1, raw_b[0], 0, 0, 512)
        cast(nc.scalar.copy, 1, raw_b[1], 512, 0, 512)
        for i in range(PIECES):
            pick(0, i)
        cast(nc.vector.tensor_copy, 1, raw_b[2], 1024, 0, 256)
        cast(nc.scalar.copy, 1, raw_b[2], 1024, 256, 512)
        cast(nc.vector.tensor_copy, 1, raw_b[3], 1536, 0, 256)
        cast(nc.vector.tensor_copy, 1, raw_b[4], 1792, 0, 160)
        cast(nc.scalar.copy, 1, raw_b[4], 1792, 160, 256)

        x_words = keep.tile([P, S], U32, name="x_words", align_bytes=64)
        x_scales = keep.tile([P, S], U8, name="x_scales", align_bytes=64)
        woven = [keep.tile([P, 2 * PIECE], U32, name="woven%d" % i, align_bytes=64) for i in range(PIECES)]

        def product(bank, j, b, c0, c1):
            m0 = b * P
            nc.tensor.matmul_mx(
                out=bank,
                lhsT=w_words[j][:, m0 : m0 + P].bitcast(FP8X4),
                lhsT_scale=w_scales[:, j * N + m0 : j * N + m0 + P],
                rhs=x_words[:, c0:c1].bitcast(FP8X4),
                rhs_scale=x_scales[:, c0:c1],
                start=True,
                stop=True,
            )

        def new_bank(name, tag):
            return psum.tile([P, BANK], F32, name=name, tag="bank%d" % tag)

        def quantise(c0, c1):
            i = c0 // PIECE
            nc.vector.quantize_mx(
                out=x_words[:, c0:c1].bitcast(FP8X4),
                scales=x_scales[:, c0:c1],
                in_=woven[i][:, 2 * (c0 - i * PIECE) : 2 * (c1 - i * PIECE)].bitcast(BF16),
            )

        def pick_and_weave(i):
            pick(1, i)
            nc.scalar.copy(woven[i][:].rearrange("p (n u) -> p n u", u=2), picked[i][:].rearrange("p (u n) -> p n u", u=2))

        rows = [[keep.tile([P, S], F32, name="rows%d_%d" % (b, j)) for j in range(3)] for b in range(2)]

        def product_rows(b, j, c0, c1, tag, copy=nc.scalar.copy):
            bank = new_bank("acc%d_%d_%d" % (b, j, c0), tag)
            product(bank[:, 0 : c1 - c0], j, b, c0, c1)
            copy(rows[b][j][:, c0:c1], bank[:, 0 : c1 - c0])

        for i in range(PIECES):
            pick_and_weave(i)
        cuts = (0, PIECE, 2 * PIECE, 3 * PIECE, S - P, S)
        for c0, c1 in zip(cuts, cuts[1:]):
            quantise(c0, c1)
        product_rows(0, 0, 0, PIECE, 0)
        product_rows(0, 0, PIECE, 2 * PIECE, 7)
        product_rows(0, 0, 2 * PIECE, 3 * PIECE, 1, nc.vector.tensor_copy)
        product_rows(0, 0, 3 * PIECE, S - P, 4)
        product_rows(0, 0, S - P, S, 2)
        product_rows(0, 1, BANK, S, 3)
        product_rows(0, 1, 0, BANK, 1)
        product_rows(0, 2, 0, BANK, 2)
        product_rows(0, 2, BANK, S, 3)

        def products1(j):
            for hf in range(2):
                product_rows(1, j, hf * BANK, (hf + 1) * BANK, 1 + (2 * j + hf) % 3)

        def centre(b, parts):
            yc = keep.tile([P, V], F32, name="yc%d" % b)
            for v0 in range(0, V, V // parts):
                v1 = v0 + V // parts
                nc.vector.tensor_copy(yc[:, v0:v1], rows[b][0][:].indirect(cen_t[:, v0 // LIST_COLS : v1 // LIST_COLS]))
            return yc

        def gates(b, yc):
            res = []
            for d in range(4):
                pre = keep.tile([P, V], F32, name="pre%d_%d" % (b, d))
                parts = 2 if (b, d) == (0, 0) else 1
                for v0 in range(0, V, V // parts):
                    v1 = v0 + V // parts
                    lst = pos_t[d][:, v0 // LIST_COLS : v1 // LIST_COLS]
                    nc.vector.tensor_tensor(pre[:, v0:v1], rows[b][1][:].indirect(lst), yc[:, v0:v1], ADD)
                gate = keep.tile([P, V], F32, name="gate%d_%d" % (b, d))
                nc.scalar.activation(gate[:], pre[:], ACT.Sigmoid)
                res.append(gate)
            return res

        def message(b, d, gate, msg, v0, v1):
            lst = pos_t[d][:, v0 // LIST_COLS : v1 // LIST_COLS]
            nc.vector.tensor_tensor(msg[:, v0:v1], rows[b][2][:].indirect(lst), gate[:, v0:v1], MULT)

        def add_turned(bank, src, v0, v1, first, last):
            for c in range(v0, v1, P):
                nc.tensor.matmul(
                    bank[:, c - v0 : c - v0 + P],
                    src[:, c : c + P],
                    ident[:],
                    start=(first and c == v0),
                    stop=(last and c + P == v1),
                    is_transpose=True,
                )

        def turn_back(name, src, width, tag):
            bank = new_bank(name, tag)
            for c in range(0, width, P):
                nc.tensor.transpose(bank[:, c : c + P], src[:, c : c + P], ident[:])
            return bank

        gates0 = gates(0, centre(0, 2))
        products1(0)
        products1(1)
        sum0 = new_bank("sum0", 0)
        for d in range(4):
            msg = keep.tile([P, V], F32, name="msg0_%d" % d, tag="rows1_0" if d == 3 else "msg0_%d" % d)
            message(0, d, gates0[d], msg, 0, V)
            add_turned(sum0, msg, 0, V, d == 0, d == 3)
            if d == 0:
                products1(2)
            if d == 2:
                yc1 = centre(1, 1)
        gates1 = gates(1, yc1)
        out0_t = keep.tile([P, V], F32, name="out0_t")
        nc.scalar.activation(out0_t[:], sum0[:], ACT.Relu)
        back0 = turn_back("back0", out0_t, V, 6)
        res0 = keep.tile([P, V], F32, name="res0")
        nc.scalar.copy(res0[:], back0[:])
        nc.sync.dma_start(out[0:P, :], res0[:])

        half = V // 2
        sum_l = [new_bank("sum_l%d" % c, 4 + c) for c in range(2)]
        sum_r = new_bank("sum_r", 7)
        msgs = [keep.tile([P, V], F32, name="msg1_%d" % d) for d in range(4)]

        def add_left(d):
            for c in range(2):
                add_turned(sum_l[c], msgs[d], c * P, (c + 1) * P, d == 0, d == 3)

        for d in range(2):
            message(1, d, gates1[d], msgs[d], 0, V)
            add_turned(sum_r, msgs[d], half, V, d == 0, False)
            add_left(d)
        message(1, 2, gates1[2], msgs[2], half, V)
        add_turned(sum_r, msgs[2], half, V, False, True)
        part_t = keep.tile([P, half], F32, name="part_t")
        nc.scalar.copy(part_t[:], sum_r[:, 0:half])
        part = turn_back("part", part_t, half, 1)
        for d in range(2, 4):
            message(1, d, gates1[d], msgs[d], 0, half)
            add_left(d)
        res_l = keep.tile([P, half], F32, name="res_l")
        left = []
        for c in range(2):
            left_t = keep.tile([P, P], F32, name="left_t%d" % c)
            nc.scalar.activation(left_t[:], sum_l[c][:, 0:P], ACT.Relu)
            left.append(turn_back("left%d" % c, left_t, P, 2 + c))
        for c in range(2):
            nc.scalar.copy(res_l[:, c * P : (c + 1) * P], left[c][:, 0:P])
        nc.scalar.dma_start(out[P : 2 * P, 0:half], res_l[:])
        for c in range(2):
            message(1, 3, gates1[3], msgs[3], half + c * P, half + (c + 1) * P)
        z = keep.tile([P, half], F32, name="z")
        res_r = keep.tile([P, half], F32, name="res_r")
        for c in range(2):
            cols = slice(c * P, (c + 1) * P)
            nc.vector.tensor_tensor(z[:, cols], msgs[3][:, half + c * P : half + (c + 1) * P], part[:, cols], ADD)
        for c in range(2):
            cols = slice(c * P, (c + 1) * P)
            nc.vector.tensor_scalar_max(res_r[:, cols], z[:, cols], 0.0)
        nc.sync.dma_start(out[P : 2 * P, half:V], res_r[:])
